import numpy as np, ml_dtypes
CORES = [3,5,19,21,35,37,51,53,67,69]
N = 10
import mx_ref
BF = ml_dtypes.bfloat16
def entries(a):
    return np.ascontiguousarray(a.T).reshape(-1)
def table(e):
    return np.ascontiguousarray(np.reshape(e, (-1, 16)).T).astype(np.int32)
def cols(t, e):
    v = np.concatenate([t.reshape(128, -1, 4), np.zeros((128, 1, 4), BF)], axis=1)
    return np.ascontiguousarray(v[:, e]).reshape(128, -1)
def f(rng, *shape):
    return mx_ref.flush((rng.standard_normal(shape, dtype=np.float32) * np.exp2(rng.integers(-2, 3, shape[:-1] + (1,)))).astype(BF))
def wide(rng, *shape, cols=0):
    v = rng.standard_normal(shape, dtype=np.float32) * np.exp2(rng.integers(-12, 13, shape)).astype(np.float32)
    if cols: v *= np.repeat(np.exp2(rng.integers(-cols, cols + 1, shape[:-2] + (1, shape[-1] // 4))) * (rng.random(shape[:-2] + (1, shape[-1] // 4)) > 0.0625), 4, axis=-1).astype(np.float32)
    return mx_ref.flush(v.astype(BF))
T, CAPP = 256, 32
def even(n):
    return [T // n + (k < T % n) for k in range(n)]
def counts(rng, h, moves=10 * N * N):
    n = np.array([[h[(d - s) % N] for d in range(N)] for s in range(N)])[rng.permutation(N)][:, rng.permutation(N)]
    top = np.where(n > 0, CAPP, 0)
    for _ in range(moves):
        a, b = rng.permutation(N)[:2]; c, e = rng.permutation(N)[:2]
        k = rng.integers(0, min(n[a, e], n[b, c], top[a, c] - n[a, c], top[b, e] - n[b, e]) + 1)
        n[a, c] += k; n[b, e] += k; n[a, e] -= k; n[b, c] -= k
    return n
def lists(rng, n, back=False):
    a = np.full((N, N, CAPP), -1)
    for s in range(N):
        p = np.arange(T)[::-1] if back else rng.permutation(T)
        for d in range(N):
            k = rng.permutation(CAPP)[:n[s, d]]
            if back: k = np.sort(k)
            a[s, d, k] = p[:n[s, d]]; p = p[n[s, d]:]
    m = []
    for d in range(N):
        k = np.flatnonzero(a[:, d].reshape(-1) >= 0)
        m.append(table(k[::-1] if back else rng.permutation(k)))
    return {"send": np.stack([table(a[s].reshape(-1)) for s in range(N)]), "mine": np.stack(m), "prev": np.stack([m[(r - 1) % N] for r in range(N)])}
def setup_inputs(rng):
    return {"x": f(rng, N, 128, 4 * T), **lists(rng, counts(rng, even(N)))}
def setup_inputs_empty(rng):
    return {**setup_inputs(rng), **lists(rng, counts(rng, even(N - 1) + [0]))}
def setup_inputs_full(rng):
    return {**setup_inputs(rng), **lists(rng, counts(rng, [min(CAPP, max(0, T - k * CAPP)) for k in range(N)], 0))}
def setup_inputs_reversed(rng):
    return {**setup_inputs(rng), **lists(rng, counts(rng, even(N)), back=True)}
def setup_inputs_spread(rng):
    d = setup_inputs(rng); d["x"] = wide(rng, N, 128, 4 * T, cols=8); return d
def check_inputs(d):
    b = []
    v = np.abs(np.asarray(d["x"]).astype(np.float32))
    if not ((v == 0) | ((v >= 2.0 ** -30) & (v <= 2.0 ** 30))).all(): b.append("x")
    for r in range(N):
        c, m = entries(d["send"][r]), entries(d["mine"][r])
        if c.min() < -1 or not np.array_equal(np.sort(c[c >= 0]), np.arange(T)): b.append("send")
        arrived = np.concatenate([entries(d["send"][s])[r * CAPP:(r + 1) * CAPP] for s in range(N)])
        if not np.array_equal(np.sort(m), np.flatnonzero(arrived >= 0)): b.append("mine")
        if not np.array_equal(d["prev"][r], d["mine"][(r - 1) % N]): b.append("prev")
    return b
def reference(x, send, mine, prev):
    K = []
    for r in range(N):
        arrived = np.concatenate([cols(x[s], entries(send[s])[r * CAPP:(r + 1) * CAPP]) for s in range(N)], axis=1)
        K.append(cols(arrived, entries(mine[r])))
    Q = [mx_ref.quantize(t) for t in K]
    y = np.zeros((N, T, 2 * T), np.float32)
    for r in range(N):
        for p in range(T // 128):
            W = mx_ref.quantize(np.ascontiguousarray(K[r][:, 512 * p:512 * p + 512]))
            y[r, 128 * p:128 * p + 128, :T] = mx_ref.matmul(W, Q[r])
            y[r, 128 * p:128 * p + 128, T:] = mx_ref.matmul(W, Q[(r - 1) % N])
    return {"y": y}

@@ -1,0 +1,262 @@
+from concourse.bass import DstId, RemoteDMATransfer, IndirectOffsetOnAxis
+from concourse.mybir import dt, AluOpType, ActivationFunctionType
+
+N = 10
+COLS = 256
+CAP = 32
+RUN = 2 * CAP
+SLOTS = N * CAP
+MOV = N * RUN
+LW = 2 * N
+BW = COLS // 16
+NOROW = 4096
+
+SCRATCH = {
+    "snd": ("sbuf", [128, LW], "int32"),
+    "soff": ("sbuf", [128, LW], "uint16"),
+    "xs": ("sbuf", [128, 4 * COLS], "bfloat16"),
+    "h": ("sbuf", [128, 4 * SLOTS], "bfloat16"),
+    "qc": ("sbuf", [128, SLOTS], "float8_e4m3fn_x4"),
+    "qs": ("sbuf", [128, SLOTS], "uint8"),
+    "mc": ("sbuf", [128, MOV], "float8_e4m3fn_x4"),
+    "ms": ("sbuf", [128, MOV], "uint8"),
+    "wc": ("sbuf", [128, 256], "float8_e4m3fn_x4"),
+    "ws": ("sbuf", [128, 256], "uint8"),
+    "lm": ("sbuf", [128, 2 * BW], "int32"),
+    "k_t": ("sbuf", [128, 2 * BW], "int32"),
+    "k_b": ("sbuf", [128, 2 * BW], "int32"),
+    "k_c": ("sbuf", [128, 2 * BW], "int32"),
+    "k_f": ("sbuf", [128, 2 * BW], "int32"),
+    "k_d": ("sbuf", [128, 2 * BW], "int32"),
+    "k_e": ("sbuf", [128, 2 * BW], "int32"),
+    "k_g": ("sbuf", [128, 2 * BW], "int32"),
+    "k_h": ("sbuf", [128, BW], "int32"),
+    "k_p": ("sbuf", [128, 2 * BW], "int32"),
+    "k_w": ("sbuf", [128, BW], "int32"),
+    "coff": ("sbuf", [128, 2 * BW], "uint16"),
+    "woff": ("sbuf", [128, BW], "uint16"),
+    "num": ("sbuf", [128, COLS], "int32"),
+    "inv": ("sbuf", [128, SLOTS], "int32"),
+    "idx": ("sbuf", [128, 4], "int32"),
+    "pp": ("psum", [128, 512 * 8], "float32"),
+}
+for _k in range(3):
+    SCRATCH["s%d" % _k] = ("sbuf", [128, MOV], "float32")
+    SCRATCH["o%d" % _k] = ("sbuf", [128, 2 * COLS], "float32")
+
+SEMAPHORES = ["l_send", "l_x", "l_lm", "l_g", "offa", "offb", "gva", "gsa", "gvb", "gsb", "qa", "qb",
+              "k1", "k2", "k3", "k4", "k5", "k6", "iot", "fil", "invd", "selfc", "r03", "r45", "r67", "r89",
+              "c0", "c1", "idxd", "sent", "stored"]
+for _k in range(3):
+    SEMAPHORES += ["mm%d%s" % (_k, _p) for _p in "eab"] + ["cp%d%s" % (_k, _p) for _p in "eab"] + ["ov%d" % _k, "os%d" % _k]
+
+
+def place(s, r):
+    u = (s - r - 5) % N
+    return u if r % 2 == 0 else u ^ 1
+
+
+def slot_pos(s, d):
+    return (d - s) % N if s % 2 else (s - 1 - d) % N
+
+
+def rank_program(g, core, T, topo):
+    r = T.rank_of(core)
+    if r is None:
+        return
+    V, S, P, Y, sem = g.vector, g.scalar, g.tensor, g.sync, T.sem
+    OP, COPY = AluOpType, ActivationFunctionType.Copy
+    rising = r % 2 == 1
+
+    for q in range(8):
+        e = S if q < 5 else Y
+        e.dma_start(T.snd[16 * q:16 * q + 16, :], T.send[:]).then_inc(sem.l_send, 16)
+    Y.dma_start(T.xs[:], T.x[:]).then_inc(sem.l_x, 16)
+    g.dma_start(T.lm[0:16, 0:BW], T.mine[:]).then_inc(sem.l_g, 16)
+    for q in range(8):
+        if q:
+            Y.dma_start(T.lm[16 * q:16 * q + 16, 0:BW], T.mine[:]).then_inc(sem.l_lm, 16)
+        Y.dma_start(T.lm[16 * q:16 * q + 16, BW:2 * BW], T.prev[:]).then_inc(sem.l_lm, 16)
+    g.iota(T.num[:], [[1, COLS]], 0, 0).then_inc(sem.iot, 1)
+
+    V.memset(T.inv[:], NOROW).then_inc(sem.fil, 1)
+    V.wait_ge(sem.l_send, 128)
+    wave = [(0, 6), (6, 10)] if rising else [(4, 10), (0, 4)]
+
+    def offsets(lo, hi, done):
+        n, k = 0, lo
+        while k < hi:
+            slot = (r + k) % N if rising else (r - 1 - k) % N
+            m = min(hi - k, N - slot if rising else slot + 1)
+            if rising:
+                V.tensor_scalar(T.soff[:, 2 * k:2 * (k + m)], T.snd[:, 2 * slot:2 * (slot + m)], 4, 0, OP.mult, OP.max).then_inc(done, 1)
+                n += 1
+            else:
+                for b in range(2):
+                    first, stop = 2 * slot + b, 2 * (slot - m + 1) + b - 1
+                    src = T.snd[:, first::-2] if stop < 0 else T.snd[:, first:stop:-2]
+                    V.tensor_scalar(T.soff[:, 2 * k + b:2 * (k + m):2], src, 4, 0, OP.mult, OP.max).then_inc(done, 1)
+                    n += 1
+            k += m
+        return n
+
+    n_off = [offsets(*wave[0], sem.offa), offsets(*wave[1], sem.offb)]
+    off_s, gv, gs, qd = [sem.offa, sem.offb], [sem.gva, sem.gvb], [sem.gsa, sem.gsb], [sem.qa, sem.qb]
+
+    for w in range(2):
+        lo, hi = wave[w]
+        for t in range(4):
+            e = V if t < 2 else S
+            if t % 2 == 0:
+                e.wait_ge(off_s[w], n_off[w])
+                if w == 0:
+                    e.wait_ge(sem.l_x, 16)
+            out = T.h[:, 128 * lo + t:128 * hi:4]
+            src = T.xs[:, t:4 * COLS].indirect(T.soff[:, 2 * lo:2 * hi])
+            if t < 2:
+                V.tensor_copy(out, src).then_inc(gv[w], 1)
+            else:
+                S.activation(out, src, COPY).then_inc(gs[w], 1)
+        V.wait_ge(gv[w], 2)
+        V.wait_ge(gs[w], 2)
+        V.quantize_mx(T.qc[:, CAP * lo:CAP * hi], T.qs[:, CAP * lo:CAP * hi], T.h[:, 128 * lo:128 * hi]).then_inc(qd[w], 1)
+
+    n_sent = 0
+    arrive = [sem.r03, sem.r03, sem.r45, sem.r67, sem.r89]
+    for w, dests in enumerate([[2, 3, 4, 5], [6, 7, 8, 9, 1]]):
+        dests = [(r + k) % N for k in dests]
+        far = [d for d in dests if topo.chip(T.cores[d]) != topo.chip(core)]
+        eng = {}
+        for i, d in enumerate(far):
+            e = topo.engines(core, T.cores[d])
+            per = len(e) // len(far)
+            eng[d] = e[per * i:per * i + per]
+        for d in dests:
+            if d not in eng:
+                used = topo.engines(core, T.cores[far[0]])
+                eng[d] = [e for e in topo.engines(core, T.cores[d]) if e not in used][:2]
+        g.wait_ge(qd[w], 1)
+        for part in range(2):
+            moves = []
+            for d in dests:
+                a = CAP * min(slot_pos(r, d), slot_pos(r, (d - 1) % N))
+                v = place(r, d)
+                rid, pid, _ = topo.addr(T.cores[d])
+                if part == 0:
+                    src, dst = T.qc[:, a:a + RUN].bitcast(dt.uint8), T.mc[:, RUN * v:RUN * v + RUN].bitcast(dt.uint8)
+                else:
+                    src, dst = T.qs[:, a:a + RUN], T.ms[:, RUN * v:RUN * v + RUN]
+                moves.append(RemoteDMATransfer(
+                    dst_ids=[DstId(rid=rid, pnc=pid)], dma_engine_mask=sum(1 << e for e in eng[d]),
+                    remote_sem=arrive[v // 2], src=src, dst=dst))
+                n_sent += len(eng[d])
+            g.remote_dma_fused(moves, local_sem=sem.sent)
+    n_03, n_45, n_67, n_89 = 16, 4, 8, 8
+
+    def copy(dc, ds, a, sc, ss, b, n, done):
+        Y.dma_start(dc[:, a:a + n].bitcast(dt.uint8), sc[:, b:b + n].bitcast(dt.uint8)).then_inc(done, 16)
+        Y.dma_start(ds[:, a:a + n], ss[:, b:b + n]).then_inc(done, 16)
+
+    def draw(pair, done):
+        copy(T.wc, T.ws, 64 * pair, T.mc, T.ms, 2 * RUN * pair + CAP, 64, done)
+
+    Y.wait_ge(sem.qa, 1)
+    Y.wait_ge(sem.qb, 1)
+    v = place(r, r)
+    own, prv = CAP * slot_pos(r, r), CAP * slot_pos(r, (r - 1) % N)
+    copy(T.mc, T.ms, RUN * v + (CAP if v % 2 == 0 else 0), T.qc, T.qs, own, CAP, sem.selfc)
+    copy(T.mc, T.ms, RUN * v + (0 if v % 2 == 0 else CAP), T.qc, T.qs, prv, CAP, sem.selfc)
+    Y.wait_ge(sem.r03, n_03)
+    draw(0, sem.c0)
+    draw(1, sem.c0)
+    Y.wait_ge(sem.invd, 1)
+    for k in range(3):
+        n = 128 if k < 2 else 64
+        Y.dma_start(T.idx[0:n, k:k + 1], T.inv[0:1, 128 * k:128 * k + n]).then_inc(sem.idxd, 16)
+    Y.wait_ge(sem.selfc, 64)
+    Y.wait_ge(sem.r45, n_45)
+    draw(2, sem.c1)
+    Y.wait_ge(sem.r67, n_67)
+    draw(3, sem.c1)
+
+    k = (r + 5) % N
+    mn, pv = slice(0, BW), slice(BW, 2 * BW)
+    V.wait_ge(sem.l_lm, 15 * 16)
+    V.wait_ge(sem.l_g, 16)
+    V.tensor_scalar(T.k_t[:], T.lm[:], CAP * k, SLOTS, OP.is_lt, OP.mult).then_inc(sem.k1, 1)
+    V.wait_ge(sem.k1, 1)
+    V.tensor_tensor(T.k_b[:], T.lm[:], T.k_t[:], OP.add).then_inc(sem.k2, 1)
+    V.wait_ge(sem.k2, 1)
+    V.tensor_scalar(T.k_c[:], T.k_b[:], CAP - 1, None, OP.bitwise_and).then_inc(sem.k3, 1)
+    V.tensor_scalar(T.k_f[:], T.k_b[:], CAP, None, OP.bitwise_and).then_inc(sem.k3, 1)
+    V.tensor_scalar(T.k_d[:], T.k_b[:], 2, -RUN * k, OP.mult, OP.add).then_inc(sem.k3, 1)
+    V.wait_ge(sem.k3, 3)
+    fo, co, fp, cp, fw, cw = (1, 0, -1, CAP, 0, 0) if r % 2 == 0 else (-3, 2 * CAP, -5, 3 * CAP, -2, CAP)
+    V.tensor_tensor(T.k_e[:], T.k_d[:], T.k_c[:], OP.subtract).then_inc(sem.k4, 1)
+    V.tensor_scalar(T.k_g[:, mn], T.k_f[:, mn], fo, co, OP.mult, OP.add).then_inc(sem.k4, 1)
+    V.tensor_scalar(T.k_g[:, pv], T.k_f[:, pv], fp, cp, OP.mult, OP.add).then_inc(sem.k4, 1)
+    V.tensor_scalar(T.k_h[:], T.k_f[:, mn], fw, cw - CAP * k, OP.mult, OP.add).then_inc(sem.k4, 1)
+    V.wait_ge(sem.k4, 4)
+    V.tensor_tensor(T.k_w[:], T.k_b[:, mn], T.k_h[:], OP.add).then_inc(sem.k5, 1)
+    V.tensor_tensor(T.k_p[:], T.k_e[:], T.k_g[:], OP.add).then_inc(sem.k5, 1)
+    V.wait_ge(sem.k5, 2)
+    V.tensor_copy(T.woff[:], T.k_w[:]).then_inc(sem.k6, 1)
+    V.tensor_copy(T.coff[:], T.k_p[:]).then_inc(sem.k6, 1)
+    V.wait_ge(sem.k6, 2)
+    V.wait_ge(sem.fil, 1)
+    V.wait_ge(sem.iot, 1)
+    V.tensor_copy(T.inv[:].indirect(T.woff[:]), T.num[:]).then_inc(sem.invd, 1)
+
+    tiles = {
+        0: (T.wc, T.ws, 0, [("e", 0, 256, 0), ("a", 256, 448, 1), ("b", 448, 640, 2)]),
+        2: (T.mc, T.ms, 4 * 2 * RUN, [("a", 0, 320, 3), ("b", 320, 640, 4)]),
+        1: (T.wc, T.ws, 128, [("a", 0, 320, 5), ("b", 320, 640, 6)]),
+    }
+
+    def product(tile, which):
+        c, s, a, parts = tiles[tile]
+        for name, lo, hi, bank in parts:
+            if name in which:
+                P.matmul_mx(T.pp[:, 512 * bank:512 * bank + hi - lo], c[:, a:a + 128], s[:, a:a + 128],
+                            T.mc[:, lo:hi], T.ms[:, lo:hi], True, True).then_inc(sem["mm%d%s" % (tile, name)], 1)
+
+    P.wait_ge(sem.r03, n_03)
+    P.wait_ge(sem.c0, 64)
+    product(0, "e")
+    P.wait_ge(sem.selfc, 64)
+    P.wait_ge(sem.r45, n_45)
+    P.wait_ge(sem.r67, n_67)
+    P.wait_ge(sem.r89, n_89)
+    product(0, "ab")
+    product(2, "ab")
+    P.wait_ge(sem.c1, 64)
+    product(1, "ab")
+
+    S.wait_ge(sem.k6, 2)
+    for tile in (0, 2, 1):
+        names = [p[0] for p in tiles[tile][3]]
+        buf, out = T["s%d" % tile], T["o%d" % tile]
+        for name, lo, hi, bank in tiles[tile][3]:
+            e = V if name == "a" else S
+            e.wait_ge(sem["mm%d%s" % (tile, name)], 1)
+            src = T.pp[:, 512 * bank:512 * bank + hi - lo]
+            done = sem["cp%d%s" % (tile, name)]
+            if name == "a":
+                V.tensor_copy(buf[:, lo:hi], src).then_inc(done, 1)
+            else:
+                S.activation(buf[:, lo:hi], src, COPY).then_inc(done, 1)
+        for name in names:
+            V.wait_ge(sem["cp%d%s" % (tile, name)], 1)
+            S.wait_ge(sem["cp%d%s" % (tile, name)], 1)
+        V.tensor_copy(out[:, 0:COLS], buf[:].indirect(T.coff[:, mn])).then_inc(sem["ov%d" % tile], 1)
+        S.activation(out[:, COLS:2 * COLS], buf[:].indirect(T.coff[:, pv]), COPY).then_inc(sem["os%d" % tile], 1)
+
+    g.wait_ge(sem.idxd, 48)
+    for tile in (0, 2, 1):
+        g.wait_ge(sem["ov%d" % tile], 1)
+        g.wait_ge(sem["os%d" % tile], 1)
+        lo, n = (0, 128) if tile < 2 else (CAP, 64)
+        g.indirect_dma_start(T.y[:], IndirectOffsetOnAxis(ap=T.idx[0:n, tile:tile + 1], axis=0),
+                             T["o%d" % tile][lo:lo + n, :], None, bounds_check=COLS - 1, oob_is_err=False).then_inc(sem.stored, 16)
+    g.wait_ge(sem.sent, n_sent)
+    g.wait_ge(sem.stored, 48)

@@ -25,39 +25,36 @@ SCRATCH = {
     "lm": ("sbuf", [128, 2 * BW], "int32"),
     "k_t": ("sbuf", [128, 2 * BW], "int32"),
     "k_b": ("sbuf", [128, 2 * BW], "int32"),
-    "k_c": ("sbuf", [128, 2 * BW], "int32"),
-    "k_f": ("sbuf", [128, 2 * BW], "int32"),
+    "k_m": ("sbuf", [128, 2 * BW], "int32"),
+    "k_f": ("sbuf", [128, BW], "int32"),
+    "k_g": ("sbuf", [128, BW], "int32"),
     "k_d": ("sbuf", [128, 2 * BW], "int32"),
     "k_e": ("sbuf", [128, 2 * BW], "int32"),
-    "k_g": ("sbuf", [128, 2 * BW], "int32"),
-    "k_h": ("sbuf", [128, BW], "int32"),
-    "k_p": ("sbuf", [128, 2 * BW], "int32"),
-    "k_w": ("sbuf", [128, BW], "int32"),
+    "k_p": ("sbuf", [128, BW], "int32"),
     "coff": ("sbuf", [128, 2 * BW], "uint16"),
     "woff": ("sbuf", [128, BW], "uint16"),
-    "num": ("sbuf", [128, COLS], "int32"),
+    "nul": ("sbuf", [128, COLS], "float32"),
+    "one": ("sbuf", [128, COLS], "float32"),
+    "num": ("sbuf", [128, COLS], "float32"),
     "inv": ("sbuf", [128, SLOTS], "int32"),
     "idx": ("sbuf", [128, 4], "int32"),
     "pp": ("psum", [128, 512 * 8], "float32"),
 }
-for _k in range(3):
-    SCRATCH["s%d" % _k] = ("sbuf", [128, MOV], "float32")
-    SCRATCH["o%d" % _k] = ("sbuf", [128, 2 * COLS], "float32")
-
 SEMAPHORES = ["l_send", "l_x", "l_lm", "l_g", "offa", "offb", "gva", "gsa", "gvb", "gsb", "qa", "qb",
-              "k1", "k2", "k3", "k4", "k5", "k6", "iot", "fil", "invd", "selfc", "r03", "r45", "r67", "r89",
-              "c0", "c1", "idxd", "sent", "stored"]
-for _k in range(3):
-    SEMAPHORES += ["mm%d%s" % (_k, _p) for _p in "eab"] + ["cp%d%s" % (_k, _p) for _p in "eab"] + ["ov%d" % _k, "os%d" % _k]
+              "k1", "k2", "k3", "k4", "k5", "k6", "k7", "cst", "fil", "numd", "invd", "selfc", "rp", "r1", "r2", "r3", "r4",
+              "ca", "cb", "idxd", "sent", "stored"]
+for _t in "dab":
+    SCRATCH["s_" + _t] = ("sbuf", [128, MOV], "float32")
+    SCRATCH["o_" + _t] = ("sbuf", [128, 2 * COLS], "float32")
+    SEMAPHORES += [_n + _t + str(_p) for _n in ("mm", "cp") for _p in range(4 if _t == "d" else 2)] + ["ov" + _t, "os" + _t]
 
 
 def place(s, r):
-    u = (s - r - 5) % N
-    return u if r % 2 == 0 else u ^ 1
+    return (s - (r - r % 2)) % N
 
 
 def slot_pos(s, d):
-    return (d - s) % N if s % 2 else (s - 1 - d) % N
+    return (s - 1 - d) % N if s % 2 else (d - s) % N
 
 
 def rank_program(g, core, T, topo):
@@ -66,10 +63,10 @@ def rank_program(g, core, T, topo):
         return
     V, S, P, Y, sem = g.vector, g.scalar, g.tensor, g.sync, T.sem
     OP, COPY = AluOpType, ActivationFunctionType.Copy
-    rising = r % 2 == 1
+    rising = r % 2 == 0
 
     for q in range(8):
-        e = S if q < 5 else Y
+        e = S if q < 4 else Y
         e.dma_start(T.snd[16 * q:16 * q + 16, :], T.send[:]).then_inc(sem.l_send, 16)
     Y.dma_start(T.xs[:], T.x[:]).then_inc(sem.l_x, 16)
     g.dma_start(T.lm[0:16, 0:BW], T.mine[:]).then_inc(sem.l_g, 16)
@@ -77,11 +74,14 @@ def rank_program(g, core, T, topo):
         if q:
             Y.dma_start(T.lm[16 * q:16 * q + 16, 0:BW], T.mine[:]).then_inc(sem.l_lm, 16)
         Y.dma_start(T.lm[16 * q:16 * q + 16, BW:2 * BW], T.prev[:]).then_inc(sem.l_lm, 16)
-    g.iota(T.num[:], [[1, COLS]], 0, 0).then_inc(sem.iot, 1)
 
+    V.memset(T.nul[:], 0.0).then_inc(sem.cst, 1)
+    V.memset(T.one[:], 1.0).then_inc(sem.cst, 1)
     V.memset(T.inv[:], NOROW).then_inc(sem.fil, 1)
+    V.wait_ge(sem.cst, 2)
+    V.tensor_tensor_scan(T.num[:], T.nul[:], T.one[:], -1.0, OP.add, OP.add).then_inc(sem.numd, 1)
     V.wait_ge(sem.l_send, 128)
-    wave = [(0, 6), (6, 10)] if rising else [(4, 10), (0, 4)]
+    stage = [(0, 4), (4, 10)] if rising else [(6, 10), (0, 6)]
 
     def offsets(lo, hi, done):
         n, k = 0, lo
@@ -100,11 +100,11 @@ def rank_program(g, core, T, topo):
             k += m
         return n
 
-    n_off = [offsets(*wave[0], sem.offa), offsets(*wave[1], sem.offb)]
+    n_off = [offsets(*stage[0], sem.offa), offsets(*stage[1], sem.offb)]
     off_s, gv, gs, qd = [sem.offa, sem.offb], [sem.gva, sem.gvb], [sem.gsa, sem.gsb], [sem.qa, sem.qb]
 
     for w in range(2):
-        lo, hi = wave[w]
+        lo, hi = stage[w]
         for t in range(4):
             e = V if t < 2 else S
             if t % 2 == 0:
@@ -121,24 +121,26 @@ def rank_program(g, core, T, topo):
         V.wait_ge(gs[w], 2)
         V.quantize_mx(T.qc[:, CAP * lo:CAP * hi], T.qs[:, CAP * lo:CAP * hi], T.h[:, 128 * lo:128 * hi]).then_inc(qd[w], 1)
 
+    others = [(r + k) % N for k in range(1, N)]
+    far = [d for d in others if topo.chip(T.cores[d]) != topo.chip(core)]
+    near = [d for d in others if d not in far]
+    arrive = {8: sem.r1, 6: sem.r2, 4: sem.r3, 2: sem.r4, 0: sem.rp}
     n_sent = 0
-    arrive = [sem.r03, sem.r03, sem.r45, sem.r67, sem.r89]
-    for w, dests in enumerate([[2, 3, 4, 5], [6, 7, 8, 9, 1]]):
-        dests = [(r + k) % N for k in dests]
-        far = [d for d in dests if topo.chip(T.cores[d]) != topo.chip(core)]
+    for w in range(4):
+        pair = far[2 * w:2 * w + 2]
         eng = {}
-        for i, d in enumerate(far):
+        for i, d in enumerate(pair):
             e = topo.engines(core, T.cores[d])
-            per = len(e) // len(far)
-            eng[d] = e[per * i:per * i + per]
-        for d in dests:
-            if d not in eng:
-                used = topo.engines(core, T.cores[far[0]])
+            eng[d] = e[len(e) // 2 * i:len(e) // 2 * (i + 1)]
+        if w == 1:
+            used = topo.engines(core, T.cores[far[0]])
+            for d in near:
                 eng[d] = [e for e in topo.engines(core, T.cores[d]) if e not in used][:2]
-        g.wait_ge(qd[w], 1)
+        if w < 2:
+            g.wait_ge(qd[w], 1)
         for part in range(2):
             moves = []
-            for d in dests:
+            for d in eng:
                 a = CAP * min(slot_pos(r, d), slot_pos(r, (d - 1) % N))
                 v = place(r, d)
                 rid, pid, _ = topo.addr(T.cores[d])
@@ -148,115 +150,114 @@ def rank_program(g, core, T, topo):
                     src, dst = T.qs[:, a:a + RUN], T.ms[:, RUN * v:RUN * v + RUN]
                 moves.append(RemoteDMATransfer(
                     dst_ids=[DstId(rid=rid, pnc=pid)], dma_engine_mask=sum(1 << e for e in eng[d]),
-                    remote_sem=arrive[v // 2], src=src, dst=dst))
+                    remote_sem=arrive[v - v % 2], src=src, dst=dst))
                 n_sent += len(eng[d])
             g.remote_dma_fused(moves, local_sem=sem.sent)
-    n_03, n_45, n_67, n_89 = 16, 4, 8, 8
+    n_wave, n_near = 16, 4
 
     def copy(dc, ds, a, sc, ss, b, n, done):
         Y.dma_start(dc[:, a:a + n].bitcast(dt.uint8), sc[:, b:b + n].bitcast(dt.uint8)).then_inc(done, 16)
         Y.dma_start(ds[:, a:a + n], ss[:, b:b + n]).then_inc(done, 16)
 
-    def draw(pair, done):
-        copy(T.wc, T.ws, 64 * pair, T.mc, T.ms, 2 * RUN * pair + CAP, 64, done)
+    def draw(a, pos, done):
+        copy(T.wc, T.ws, a, T.mc, T.ms, RUN * pos + CAP, 64, done)
 
     Y.wait_ge(sem.qa, 1)
     Y.wait_ge(sem.qb, 1)
     v = place(r, r)
     own, prv = CAP * slot_pos(r, r), CAP * slot_pos(r, (r - 1) % N)
-    copy(T.mc, T.ms, RUN * v + (CAP if v % 2 == 0 else 0), T.qc, T.qs, own, CAP, sem.selfc)
-    copy(T.mc, T.ms, RUN * v + (0 if v % 2 == 0 else CAP), T.qc, T.qs, prv, CAP, sem.selfc)
-    Y.wait_ge(sem.r03, n_03)
-    draw(0, sem.c0)
-    draw(1, sem.c0)
-    Y.wait_ge(sem.invd, 1)
-    for k in range(3):
-        n = 128 if k < 2 else 64
-        Y.dma_start(T.idx[0:n, k:k + 1], T.inv[0:1, 128 * k:128 * k + n]).then_inc(sem.idxd, 16)
+    copy(T.mc, T.ms, RUN * v + (CAP if rising else 0), T.qc, T.qs, own, CAP, sem.selfc)
+    copy(T.mc, T.ms, RUN * v + (0 if rising else CAP), T.qc, T.qs, prv, CAP, sem.selfc)
+    Y.wait_ge(sem.r2, n_wave)
+    draw(64, 6, sem.ca)
     Y.wait_ge(sem.selfc, 64)
-    Y.wait_ge(sem.r45, n_45)
-    draw(2, sem.c1)
-    Y.wait_ge(sem.r67, n_67)
-    draw(3, sem.c1)
+    Y.wait_ge(sem.rp, n_near)
+    draw(0, 0, sem.ca)
+    Y.wait_ge(sem.r3, n_wave)
+    draw(192, 4, sem.cb)
+    Y.wait_ge(sem.r4, n_wave)
+    draw(128, 2, sem.cb)
 
-    k = (r + 5) % N
+    base = r - r % 2
     mn, pv = slice(0, BW), slice(BW, 2 * BW)
     V.wait_ge(sem.l_lm, 15 * 16)
     V.wait_ge(sem.l_g, 16)
-    V.tensor_scalar(T.k_t[:], T.lm[:], CAP * k, SLOTS, OP.is_lt, OP.mult).then_inc(sem.k1, 1)
+    V.tensor_scalar(T.k_t[:], T.lm[:], CAP * base, SLOTS, OP.is_lt, OP.mult).then_inc(sem.k1, 1)
     V.wait_ge(sem.k1, 1)
     V.tensor_tensor(T.k_b[:], T.lm[:], T.k_t[:], OP.add).then_inc(sem.k2, 1)
     V.wait_ge(sem.k2, 1)
-    V.tensor_scalar(T.k_c[:], T.k_b[:], CAP - 1, None, OP.bitwise_and).then_inc(sem.k3, 1)
-    V.tensor_scalar(T.k_f[:], T.k_b[:], CAP, None, OP.bitwise_and).then_inc(sem.k3, 1)
-    V.tensor_scalar(T.k_d[:], T.k_b[:], 2, -RUN * k, OP.mult, OP.add).then_inc(sem.k3, 1)
-    V.wait_ge(sem.k3, 3)
-    fo, co, fp, cp, fw, cw = (1, 0, -1, CAP, 0, 0) if r % 2 == 0 else (-3, 2 * CAP, -5, 3 * CAP, -2, CAP)
-    V.tensor_tensor(T.k_e[:], T.k_d[:], T.k_c[:], OP.subtract).then_inc(sem.k4, 1)
-    V.tensor_scalar(T.k_g[:, mn], T.k_f[:, mn], fo, co, OP.mult, OP.add).then_inc(sem.k4, 1)
-    V.tensor_scalar(T.k_g[:, pv], T.k_f[:, pv], fp, cp, OP.mult, OP.add).then_inc(sem.k4, 1)
-    V.tensor_scalar(T.k_h[:], T.k_f[:, mn], fw, cw - CAP * k, OP.mult, OP.add).then_inc(sem.k4, 1)
-    V.wait_ge(sem.k4, 4)
-    V.tensor_tensor(T.k_w[:], T.k_b[:, mn], T.k_h[:], OP.add).then_inc(sem.k5, 1)
-    V.tensor_tensor(T.k_p[:], T.k_e[:], T.k_g[:], OP.add).then_inc(sem.k5, 1)
-    V.wait_ge(sem.k5, 2)
-    V.tensor_copy(T.woff[:], T.k_w[:]).then_inc(sem.k6, 1)
-    V.tensor_copy(T.coff[:], T.k_p[:]).then_inc(sem.k6, 1)
-    V.wait_ge(sem.k6, 2)
+    V.tensor_scalar(T.woff[:], T.k_b[:, mn], -CAP * base, None, OP.add).then_inc(sem.k3, 1)
+    V.wait_ge(sem.k3, 1)
     V.wait_ge(sem.fil, 1)
-    V.wait_ge(sem.iot, 1)
+    V.wait_ge(sem.numd, 1)
     V.tensor_copy(T.inv[:].indirect(T.woff[:]), T.num[:]).then_inc(sem.invd, 1)
+    V.tensor_scalar(T.k_m[:], T.k_b[:], RUN - 1, None, OP.bitwise_and).then_inc(sem.k4, 1)
+    V.tensor_scalar(T.k_f[:], T.k_b[:, pv], CAP, None, OP.bitwise_and).then_inc(sem.k4, 1)
+    V.tensor_scalar(T.k_d[:], T.k_b[:], 2, -RUN * base, OP.mult, OP.add).then_inc(sem.k4, 1)
+    V.wait_ge(sem.k4, 3)
+    V.tensor_tensor(T.k_e[:], T.k_d[:], T.k_m[:], OP.subtract).then_inc(sem.k5, 1)
+    V.tensor_scalar(T.k_g[:], T.k_f[:], 2, None, OP.mult).then_inc(sem.k5, 1)
+    V.wait_ge(sem.k5, 2)
+    V.tensor_tensor(T.k_p[:], T.k_e[:, pv], T.k_g[:], OP.add).then_inc(sem.k6, 1)
+    V.tensor_scalar(T.coff[:, mn], T.k_e[:, mn], CAP, None, OP.add).then_inc(sem.k7, 1)
+    V.wait_ge(sem.k6, 1)
+    V.tensor_copy(T.coff[:, pv], T.k_p[:]).then_inc(sem.k7, 1)
+
+    S.wait_ge(sem.invd, 1)
+    for col, p, a, n in ((0, 0, 256, 64), (1, 0, 0, 64), (1, 64, 192, 64), (2, 0, 64, 128)):
+        S.dma_start(T.idx[p:p + n, col:col + 1], T.inv[0:1, a:a + n]).then_inc(sem.idxd, 16)
 
     tiles = {
-        0: (T.wc, T.ws, 0, [("e", 0, 256, 0), ("a", 256, 448, 1), ("b", 448, 640, 2)]),
-        2: (T.mc, T.ms, 4 * 2 * RUN, [("a", 0, 320, 3), ("b", 320, 640, 4)]),
-        1: (T.wc, T.ws, 128, [("a", 0, 320, 5), ("b", 320, 640, 6)]),
+        "d": (T.mc, T.ms, 8 * RUN, [(6 * RUN, 10 * RUN, 0, S), (0, 2 * RUN, 1, V), (4 * RUN, 6 * RUN, 2, S), (2 * RUN, 4 * RUN, 3, V)]),
+        "a": (T.wc, T.ws, 0, [(0, 5 * RUN, 4, V), (5 * RUN, 10 * RUN, 5, S)]),
+        "b": (T.wc, T.ws, 128, [(0, 5 * RUN, 6, V), (5 * RUN, 10 * RUN, 7, S)]),
     }
 
-    def product(tile, which):
+    def product(tile, i):
         c, s, a, parts = tiles[tile]
-        for name, lo, hi, bank in parts:
-            if name in which:
-                P.matmul_mx(T.pp[:, 512 * bank:512 * bank + hi - lo], c[:, a:a + 128], s[:, a:a + 128],
-                            T.mc[:, lo:hi], T.ms[:, lo:hi], True, True).then_inc(sem["mm%d%s" % (tile, name)], 1)
+        lo, hi, bank, _ = parts[i]
+        P.matmul_mx(T.pp[:, 512 * bank:512 * bank + hi - lo], c[:, a:a + 128], s[:, a:a + 128],
+                    T.mc[:, lo:hi], T.ms[:, lo:hi], True, True).then_inc(sem["mm%s%d" % (tile, i)], 1)
 
-    P.wait_ge(sem.r03, n_03)
-    P.wait_ge(sem.c0, 64)
-    product(0, "e")
+    P.wait_ge(sem.r1, n_wave)
+    P.wait_ge(sem.r2, n_wave)
+    product("d", 0)
     P.wait_ge(sem.selfc, 64)
-    P.wait_ge(sem.r45, n_45)
-    P.wait_ge(sem.r67, n_67)
-    P.wait_ge(sem.r89, n_89)
-    product(0, "ab")
-    product(2, "ab")
-    P.wait_ge(sem.c1, 64)
-    product(1, "ab")
+    P.wait_ge(sem.rp, n_near)
+    product("d", 1)
+    P.wait_ge(sem.r3, n_wave)
+    product("d", 2)
+    P.wait_ge(sem.r4, n_wave)
+    product("d", 3)
+    for tile, done in (("a", sem.ca), ("b", sem.cb)):
+        P.wait_ge(done, 64)
+        product(tile, 0)
+        product(tile, 1)
 
-    S.wait_ge(sem.k6, 2)
-    for tile in (0, 2, 1):
-        names = [p[0] for p in tiles[tile][3]]
-        buf, out = T["s%d" % tile], T["o%d" % tile]
-        for name, lo, hi, bank in tiles[tile][3]:
-            e = V if name == "a" else S
-            e.wait_ge(sem["mm%d%s" % (tile, name)], 1)
+    V.wait_ge(sem.k7, 2)
+    S.wait_ge(sem.k7, 2)
+    for tile in "dab":
+        parts = tiles[tile][3]
+        buf, out = T["s_" + tile], T["o_" + tile]
+        for i, (lo, hi, bank, e) in enumerate(parts):
+            e.wait_ge(sem["mm%s%d" % (tile, i)], 1)
             src = T.pp[:, 512 * bank:512 * bank + hi - lo]
-            done = sem["cp%d%s" % (tile, name)]
-            if name == "a":
+            done = sem["cp%s%d" % (tile, i)]
+            if e is V:
                 V.tensor_copy(buf[:, lo:hi], src).then_inc(done, 1)
             else:
                 S.activation(buf[:, lo:hi], src, COPY).then_inc(done, 1)
-        for name in names:
-            V.wait_ge(sem["cp%d%s" % (tile, name)], 1)
-            S.wait_ge(sem["cp%d%s" % (tile, name)], 1)
-        V.tensor_copy(out[:, 0:COLS], buf[:].indirect(T.coff[:, mn])).then_inc(sem["ov%d" % tile], 1)
-        S.activation(out[:, COLS:2 * COLS], buf[:].indirect(T.coff[:, pv]), COPY).then_inc(sem["os%d" % tile], 1)
+        for i in range(len(parts)):
+            V.wait_ge(sem["cp%s%d" % (tile, i)], 1)
+            S.wait_ge(sem["cp%s%d" % (tile, i)], 1)
+        V.tensor_copy(out[:, 0:COLS], buf[:].indirect(T.coff[:, mn])).then_inc(sem["ov" + tile], 1)
+        S.activation(out[:, COLS:2 * COLS], buf[:].indirect(T.coff[:, pv]), COPY).then_inc(sem["os" + tile], 1)
 
-    g.wait_ge(sem.idxd, 48)
-    for tile in (0, 2, 1):
-        g.wait_ge(sem["ov%d" % tile], 1)
-        g.wait_ge(sem["os%d" % tile], 1)
-        lo, n = (0, 128) if tile < 2 else (CAP, 64)
-        g.indirect_dma_start(T.y[:], IndirectOffsetOnAxis(ap=T.idx[0:n, tile:tile + 1], axis=0),
-                             T["o%d" % tile][lo:lo + n, :], None, bounds_check=COLS - 1, oob_is_err=False).then_inc(sem.stored, 16)
+    g.wait_ge(sem.idxd, 64)
+    for col, (tile, lo, n) in enumerate((("d", CAP, 64), ("a", 0, 128), ("b", 0, 128))):
+        g.wait_ge(sem["ov" + tile], 1)
+        g.wait_ge(sem["os" + tile], 1)
+        g.indirect_dma_start(T.y[:], IndirectOffsetOnAxis(ap=T.idx[0:n, col:col + 1], axis=0),
+                             T["o_" + tile][lo:lo + n, :], None, bounds_check=COLS - 1, oob_is_err=False).then_inc(sem.stored, 16)
     g.wait_ge(sem.sent, n_sent)
     g.wait_ge(sem.stored, 48)

from concourse.bass import DstId, RemoteDMATransfer, IndirectOffsetOnAxis
from concourse.mybir import dt, AluOpType, ActivationFunctionType

N = 10
COLS = 256
CAP = 32
RUN = 2 * CAP
SLOTS = N * CAP
MOV = N * RUN
LW = 2 * N
BW = COLS // 16
NOROW = 4096

SCRATCH = {
    "snd": ("sbuf", [128, LW], "int32"),
    "soff": ("sbuf", [128, LW], "uint16"),
    "xs": ("sbuf", [128, 4 * COLS], "bfloat16"),
    "h": ("sbuf", [128, 4 * SLOTS], "bfloat16"),
    "qc": ("sbuf", [128, SLOTS], "float8_e4m3fn_x4"),
    "qs": ("sbuf", [128, SLOTS], "uint8"),
    "mc": ("sbuf", [128, MOV], "float8_e4m3fn_x4"),
    "ms": ("sbuf", [128, MOV], "uint8"),
    "wc": ("sbuf", [128, 256], "float8_e4m3fn_x4"),
    "ws": ("sbuf", [128, 256], "uint8"),
    "lm": ("sbuf", [128, 2 * BW], "int32"),
    "k_t": ("sbuf", [128, 2 * BW], "int32"),
    "k_b": ("sbuf", [128, 2 * BW], "int32"),
    "k_m": ("sbuf", [128, 2 * BW], "int32"),
    "k_f": ("sbuf", [128, BW], "int32"),
    "k_g": ("sbuf", [128, BW], "int32"),
    "k_d": ("sbuf", [128, 2 * BW], "int32"),
    "k_e": ("sbuf", [128, 2 * BW], "int32"),
    "k_p": ("sbuf", [128, BW], "int32"),
    "coff": ("sbuf", [128, 2 * BW], "uint16"),
    "woff": ("sbuf", [128, BW], "uint16"),
    "nul": ("sbuf", [128, COLS], "float32"),
    "one": ("sbuf", [128, COLS], "float32"),
    "num": ("sbuf", [128, COLS], "float32"),
    "inv": ("sbuf", [128, SLOTS], "int32"),
    "idx": ("sbuf", [128, 4], "int32"),
    "pp": ("psum", [128, 512 * 8], "float32"),
}
SEMAPHORES = ["l_send", "l_x", "l_lm", "l_g", "offa", "offb", "gva", "gsa", "gvb", "gsb", "qa", "qb",
              "k1", "k2", "k3", "k4", "k5", "k6", "k7", "cst", "fil", "numd", "invd", "selfc", "rp", "r1", "r2", "r3", "r4",
              "ca", "cb", "idxd", "sent", "stored"]
for _t in "dab":
    SCRATCH["s_" + _t] = ("sbuf", [128, MOV], "float32")
    SCRATCH["o_" + _t] = ("sbuf", [128, 2 * COLS], "float32")
    SEMAPHORES += [_n + _t + str(_p) for _n in ("mm", "cp") for _p in range(4 if _t == "d" else 2)] + ["ov" + _t, "os" + _t]


def place(s, r):
    return (s - (r - r % 2)) % N


def slot_pos(s, d):
    return (s - 1 - d) % N if s % 2 else (d - s) % N


def rank_program(g, core, T, topo):
    r = T.rank_of(core)
    if r is None:
        return
    V, S, P, Y, sem = g.vector, g.scalar, g.tensor, g.sync, T.sem
    OP, COPY = AluOpType, ActivationFunctionType.Copy
    rising = r % 2 == 0

    for q in range(8):
        e = S if q < 4 else Y
        e.dma_start(T.snd[16 * q:16 * q + 16, :], T.send[:]).then_inc(sem.l_send, 16)
    Y.dma_start(T.xs[:], T.x[:]).then_inc(sem.l_x, 16)
    g.dma_start(T.lm[0:16, 0:BW], T.mine[:]).then_inc(sem.l_g, 16)
    for q in range(8):
        if q:
            Y.dma_start(T.lm[16 * q:16 * q + 16, 0:BW], T.mine[:]).then_inc(sem.l_lm, 16)
        Y.dma_start(T.lm[16 * q:16 * q + 16, BW:2 * BW], T.prev[:]).then_inc(sem.l_lm, 16)

    V.memset(T.nul[:], 0.0).then_inc(sem.cst, 1)
    V.memset(T.one[:], 1.0).then_inc(sem.cst, 1)
    V.memset(T.inv[:], NOROW).then_inc(sem.fil, 1)
    V.wait_ge(sem.cst, 2)
    V.tensor_tensor_scan(T.num[:], T.nul[:], T.one[:], -1.0, OP.add, OP.add).then_inc(sem.numd, 1)
    V.wait_ge(sem.l_send, 128)
    stage = [(0, 4), (4, 10)] if rising else [(6, 10), (0, 6)]

    def offsets(lo, hi, done):
        n, k = 0, lo
        while k < hi:
            slot = (r + k) % N if rising else (r - 1 - k) % N
            m = min(hi - k, N - slot if rising else slot + 1)
            if rising:
                V.tensor_scalar(T.soff[:, 2 * k:2 * (k + m)], T.snd[:, 2 * slot:2 * (slot + m)], 4, 0, OP.mult, OP.max).then_inc(done, 1)
                n += 1
            else:
                for b in range(2):
                    first, stop = 2 * slot + b, 2 * (slot - m + 1) + b - 1
                    src = T.snd[:, first::-2] if stop < 0 else T.snd[:, first:stop:-2]
                    V.tensor_scalar(T.soff[:, 2 * k + b:2 * (k + m):2], src, 4, 0, OP.mult, OP.max).then_inc(done, 1)
                    n += 1
            k += m
        return n

    n_off = [offsets(*stage[0], sem.offa), offsets(*stage[1], sem.offb)]
    off_s, gv, gs, qd = [sem.offa, sem.offb], [sem.gva, sem.gvb], [sem.gsa, sem.gsb], [sem.qa, sem.qb]

    for w in range(2):
        lo, hi = stage[w]
        for t in range(4):
            e = V if t < 2 else S
            if t % 2 == 0:
                e.wait_ge(off_s[w], n_off[w])
                if w == 0:
                    e.wait_ge(sem.l_x, 16)
            out = T.h[:, 128 * lo + t:128 * hi:4]
            src = T.xs[:, t:4 * COLS].indirect(T.soff[:, 2 * lo:2 * hi])
            if t < 2:
                V.tensor_copy(out, src).then_inc(gv[w], 1)
            else:
                S.activation(out, src, COPY).then_inc(gs[w], 1)
        V.wait_ge(gv[w], 2)
        V.wait_ge(gs[w], 2)
        V.quantize_mx(T.qc[:, CAP * lo:CAP * hi], T.qs[:, CAP * lo:CAP * hi], T.h[:, 128 * lo:128 * hi]).then_inc(qd[w], 1)

    others = [(r + k) % N for k in range(1, N)]
    far = [d for d in others if topo.chip(T.cores[d]) != topo.chip(core)]
    near = [d for d in others if d not in far]
    arrive = {8: sem.r1, 6: sem.r2, 4: sem.r3, 2: sem.r4, 0: sem.rp}
    n_sent = 0
    for w in range(4):
        pair = far[2 * w:2 * w + 2]
        eng = {}
        for i, d in enumerate(pair):
            e = topo.engines(core, T.cores[d])
            eng[d] = e[len(e) // 2 * i:len(e) // 2 * (i + 1)]
        if w == 1:
            used = topo.engines(core, T.cores[far[0]])
            for d in near:
                eng[d] = [e for e in topo.engines(core, T.cores[d]) if e not in used][:2]
        if w < 2:
            g.wait_ge(qd[w], 1)
        for part in range(2):
            moves = []
            for d in eng:
                a = CAP * min(slot_pos(r, d), slot_pos(r, (d - 1) % N))
                v = place(r, d)
                rid, pid, _ = topo.addr(T.cores[d])
                if part == 0:
                    src, dst = T.qc[:, a:a + RUN].bitcast(dt.uint8), T.mc[:, RUN * v:RUN * v + RUN].bitcast(dt.uint8)
                else:
                    src, dst = T.qs[:, a:a + RUN], T.ms[:, RUN * v:RUN * v + RUN]
                moves.append(RemoteDMATransfer(
                    dst_ids=[DstId(rid=rid, pnc=pid)], dma_engine_mask=sum(1 << e for e in eng[d]),
                    remote_sem=arrive[v - v % 2], src=src, dst=dst))
                n_sent += len(eng[d])
            g.remote_dma_fused(moves, local_sem=sem.sent)
    n_wave, n_near = 16, 4

    def copy(dc, ds, a, sc, ss, b, n, done):
        Y.dma_start(dc[:, a:a + n].bitcast(dt.uint8), sc[:, b:b + n].bitcast(dt.uint8)).then_inc(done, 16)
        Y.dma_start(ds[:, a:a + n], ss[:, b:b + n]).then_inc(done, 16)

    def draw(a, pos, done):
        copy(T.wc, T.ws, a, T.mc, T.ms, RUN * pos + CAP, 64, done)

    Y.wait_ge(sem.qa, 1)
    Y.wait_ge(sem.qb, 1)
    v = place(r, r)
    own, prv = CAP * slot_pos(r, r), CAP * slot_pos(r, (r - 1) % N)
    copy(T.mc, T.ms, RUN * v + (CAP if rising else 0), T.qc, T.qs, own, CAP, sem.selfc)
    copy(T.mc, T.ms, RUN * v + (0 if rising else CAP), T.qc, T.qs, prv, CAP, sem.selfc)
    Y.wait_ge(sem.r2, n_wave)
    draw(64, 6, sem.ca)
    Y.wait_ge(sem.selfc, 64)
    Y.wait_ge(sem.rp, n_near)
    draw(0, 0, sem.ca)
    Y.wait_ge(sem.r3, n_wave)
    draw(192, 4, sem.cb)
    Y.wait_ge(sem.r4, n_wave)
    draw(128, 2, sem.cb)

    base = r - r % 2
    mn, pv = slice(0, BW), slice(BW, 2 * BW)
    V.wait_ge(sem.l_lm, 15 * 16)
    V.wait_ge(sem.l_g, 16)
    V.tensor_scalar(T.k_t[:], T.lm[:], CAP * base, SLOTS, OP.is_lt, OP.mult).then_inc(sem.k1, 1)
    V.wait_ge(sem.k1, 1)
    V.tensor_tensor(T.k_b[:], T.lm[:], T.k_t[:], OP.add).then_inc(sem.k2, 1)
    V.wait_ge(sem.k2, 1)
    V.tensor_scalar(T.woff[:], T.k_b[:, mn], -CAP * base, None, OP.add).then_inc(sem.k3, 1)
    V.wait_ge(sem.k3, 1)
    V.wait_ge(sem.fil, 1)
    V.wait_ge(sem.numd, 1)
    V.tensor_copy(T.inv[:].indirect(T.woff[:]), T.num[:]).then_inc(sem.invd, 1)
    V.tensor_scalar(T.k_m[:], T.k_b[:], RUN - 1, None, OP.bitwise_and).then_inc(sem.k4, 1)
    V.tensor_scalar(T.k_f[:], T.k_b[:, pv], CAP, None, OP.bitwise_and).then_inc(sem.k4, 1)
    V.tensor_scalar(T.k_d[:], T.k_b[:], 2, -RUN * base, OP.mult, OP.add).then_inc(sem.k4, 1)
    V.wait_ge(sem.k4, 3)
    V.tensor_tensor(T.k_e[:], T.k_d[:], T.k_m[:], OP.subtract).then_inc(sem.k5, 1)
    V.tensor_scalar(T.k_g[:], T.k_f[:], 2, None, OP.mult).then_inc(sem.k5, 1)
    V.wait_ge(sem.k5, 2)
    V.tensor_tensor(T.k_p[:], T.k_e[:, pv], T.k_g[:], OP.add).then_inc(sem.k6, 1)
    V.tensor_scalar(T.coff[:, mn], T.k_e[:, mn], CAP, None, OP.add).then_inc(sem.k7, 1)
    V.wait_ge(sem.k6, 1)
    V.tensor_copy(T.coff[:, pv], T.k_p[:]).then_inc(sem.k7, 1)

    S.wait_ge(sem.invd, 1)
    for col, p, a, n in ((0, 0, 256, 64), (1, 0, 0, 64), (1, 64, 192, 64), (2, 0, 64, 128)):
        S.dma_start(T.idx[p:p + n, col:col + 1], T.inv[0:1, a:a + n]).then_inc(sem.idxd, 16)

    tiles = {
        "d": (T.mc, T.ms, 8 * RUN, [(6 * RUN, 10 * RUN, 0, S), (0, 2 * RUN, 1, V), (4 * RUN, 6 * RUN, 2, S), (2 * RUN, 4 * RUN, 3, V)]),
        "a": (T.wc, T.ws, 0, [(0, 5 * RUN, 4, V), (5 * RUN, 10 * RUN, 5, S)]),
        "b": (T.wc, T.ws, 128, [(0, 5 * RUN, 6, V), (5 * RUN, 10 * RUN, 7, S)]),
    }

    def product(tile, i):
        c, s, a, parts = tiles[tile]
        lo, hi, bank, _ = parts[i]
        P.matmul_mx(T.pp[:, 512 * bank:512 * bank + hi - lo], c[:, a:a + 128], s[:, a:a + 128],
                    T.mc[:, lo:hi], T.ms[:, lo:hi], True, True).then_inc(sem["mm%s%d" % (tile, i)], 1)

    P.wait_ge(sem.r1, n_wave)
    P.wait_ge(sem.r2, n_wave)
    product("d", 0)
    P.wait_ge(sem.selfc, 64)
    P.wait_ge(sem.rp, n_near)
    product("d", 1)
    P.wait_ge(sem.r3, n_wave)
    product("d", 2)
    P.wait_ge(sem.r4, n_wave)
    product("d", 3)
    for tile, done in (("a", sem.ca), ("b", sem.cb)):
        P.wait_ge(done, 64)
        product(tile, 0)
        product(tile, 1)

    V.wait_ge(sem.k7, 2)
    S.wait_ge(sem.k7, 2)
    for tile in "dab":
        parts = tiles[tile][3]
        buf, out = T["s_" + tile], T["o_" + tile]
        for i, (lo, hi, bank, e) in enumerate(parts):
            e.wait_ge(sem["mm%s%d" % (tile, i)], 1)
            src = T.pp[:, 512 * bank:512 * bank + hi - lo]
            done = sem["cp%s%d" % (tile, i)]
            if e is V:
                V.tensor_copy(buf[:, lo:hi], src).then_inc(done, 1)
            else:
                S.activation(buf[:, lo:hi], src, COPY).then_inc(done, 1)
        for i in range(len(parts)):
            V.wait_ge(sem["cp%s%d" % (tile, i)], 1)
            S.wait_ge(sem["cp%s%d" % (tile, i)], 1)
        V.tensor_copy(out[:, 0:COLS], buf[:].indirect(T.coff[:, mn])).then_inc(sem["ov" + tile], 1)
        S.activation(out[:, COLS:2 * COLS], buf[:].indirect(T.coff[:, pv]), COPY).then_inc(sem["os" + tile], 1)

    g.wait_ge(sem.idxd, 64)
    for col, (tile, lo, n) in enumerate((("d", CAP, 64), ("a", 0, 128), ("b", 0, 128))):
        g.wait_ge(sem["ov" + tile], 1)
        g.wait_ge(sem["os" + tile], 1)
        g.indirect_dma_start(T.y[:], IndirectOffsetOnAxis(ap=T.idx[0:n, col:col + 1], axis=0),
                             T["o_" + tile][lo:lo + n, :], None, bounds_check=COLS - 1, oob_is_err=False).then_inc(sem.stored, 16)
    g.wait_ge(sem.sent, n_sent)
    g.wait_ge(sem.stored, 48)
